import numpy as np, ml_dtypes
CORES = [9,41,49,65,73,81,97,113,15,47,55,71,79,87,103,119]
N = 16
import mx_ref
NC, G, GR = 256, 4, 4
C = np.float32(0.031)
BF = ml_dtypes.bfloat16
def cut(t, i, w=512):
    return t[:, w * i:w * i + w]
def tile(rs):
    return np.stack(rs, axis=2).reshape(128, -1).astype(BF)
def layer(w, X):
    out = []
    for i in range(G):
        for t in range(len(X)):
            p = mx_ref.matmul(mx_ref.quantize(cut(w, len(X) * i + t)), X[t])
            z = p if t == 0 else z + p
        out.append(z)
    return out
def act(Z):
    return [np.maximum(z, 0) * C for z in Z]
def setup_inputs(rng):
    def f(*shape):
        return mx_ref.flush((rng.standard_normal(shape, dtype=np.float32) * np.exp2(rng.integers(-2, 3, shape[:-1] + (1,)))).astype(BF))
    return {"xa": f(N, 128, 512), "xb": f(N, 128, 4 * NC), "wa": f(N, 128, G * 512), "wb": f(N, 128, G * 512)}
def setup_inputs_blocks(rng):
    d = setup_inputs(rng)
    for k in ("xa", "xb", "wa", "wb"): d[k] = mx_ref.spread(d[k], rng, 2)
    return d
def setup_inputs_wide(rng):
    d = setup_inputs(rng)
    for k in ("xa", "xb", "wa", "wb"): d[k] = mx_ref.flush((d[k].astype(np.float32) * np.exp2(rng.integers(-5, 6, (N, 1, 1))).astype(np.float32)).astype(BF))
    return d
def reference(xa, xb, wa, wb):
    A = [mx_ref.quantize(tile(act(layer(wa[j], [mx_ref.quantize(xa[j])])))) for j in range(N)]
    M = [mx_ref.quantize(tile(act(layer(wb[j], [mx_ref.quantize(xb[j])])))) for j in range(N)]
    y = np.zeros((N, 128, NC), np.float32)
    for r in range(N):
        i, j = divmod(r, GR)
        for k in range(GR):
            p = mx_ref.matmul(A[GR * i + k], M[GR * k + j])
            y[r] = p if k == 0 else y[r] + p
    return {"y": y}

@@ -1,0 +1,221 @@
+from concourse.bass import DstId, RemoteDMATransfer
+from concourse.mybir import dt, AluOpType, ActivationFunctionType
+
+N, G, GR = 16, 4, 4
+SIM_CORES = 128
+SCALE = 0.031
+COLS = {"a": 128, "b": 256}
+FIRST = 3
+RELAYED = 2
+ORDER = "ab"
+
+SCRATCH = {"ysb": ("sbuf", [128, 256], "float32")}
+SEMAPHORES = ["sent", "mmy", "cpy", "sty"]
+for _q in "ab":
+    _n = COLS[_q]
+    SCRATCH["tx" + _q] = ("sbuf", [128, 4 * _n], "bfloat16")
+    SCRATCH["tw" + _q] = ("sbuf", [128, 512 * G], "bfloat16")
+    SCRATCH["cx" + _q] = ("sbuf", [128, _n], "float8_e4m3fn_x4")
+    SCRATCH["sx" + _q] = ("sbuf", [128, _n], "uint8")
+    SCRATCH["cw" + _q] = ("sbuf", [128, 128 * G], "float8_e4m3fn_x4")
+    SCRATCH["sw" + _q] = ("sbuf", [128, 128 * G], "uint8")
+    SCRATCH["t" + _q] = ("sbuf", [128, 4 * _n], "bfloat16")
+    SCRATCH["ps" + _q] = ("psum", [128, 512 * G], "float32")
+    for _k in range(GR):
+        SCRATCH["%sc%d" % (_q, _k)] = ("sbuf", [128, _n], "float8_e4m3fn_x4")
+        SCRATCH["%ss%d" % (_q, _k)] = ("sbuf", [128, _n], "uint8")
+        SEMAPHORES += ["%sc%d" % (_q, _k), "%ss%d" % (_q, _k)]
+    SEMAPHORES += [s + _q for s in ("lx", "lw0", "lw1", "qx", "act", "q")]
+    SEMAPHORES += ["%s%s%d" % (s, _q, i) for s in ("qw", "mm") for i in range(G)]
+
+
+def slot(kind, r):
+    return r % GR if kind == "a" else r // GR
+
+
+def engines(mask):
+    return bin(mask).count("1")
+
+
+def near(ranks, src, dst, topo):
+    return [h for h in range(SIM_CORES) if h not in ranks and topo.chip(h) == topo.chip(src)
+            and topo.die(h) == topo.die(src) and topo.may_write(h, dst)]
+
+
+def far(ranks, src, dst, topo):
+    return [h for h in range(SIM_CORES) if h not in ranks and topo.mates(topo.chip(h), topo.chip(dst))
+            and topo.same_plane(topo.chip(h), topo.chip(src)) and topo.die(h) == topo.die(src)
+            and topo.may_write(h, dst)]
+
+
+def roads_a(ranks, src, dsts, topo):
+    away = [d for d in dsts if not topo.same_plane(topo.chip(src), topo.chip(d))]
+    rest = [d for d in dsts if d not in away]
+    by = {}
+    for d in away + rest:
+        hs = [h for h in near(ranks, src, d, topo) if h not in by.values()]
+        hs.sort(key=lambda h: (away != [] and topo.may_write(h, away[0])) != (d in away))
+        if hs and len(by) < RELAYED:
+            by[d] = hs[0]
+        elif not topo.may_write(src, d):
+            by[d] = far(ranks, src, d, topo)[0]
+    return {d: [by[d]] if d in by else [] for d in dsts}
+
+
+def roads_b(ranks, src, dsts, topo):
+    ways = {}
+    for d in dsts:
+        if topo.chip(d) == topo.chip(src):
+            ways[d] = []
+        elif topo.die(d) == topo.die(src):
+            ways[d] = [] if topo.may_write(src, d) else [near(ranks, src, d, topo)[0]]
+        else:
+            twin = [e for e in dsts if e != d and topo.chip(e) == topo.chip(d)][0]
+            ways[d] = [twin] if topo.may_write(src, d) else [far(ranks, src, d, topo)[0]]
+    return ways
+
+
+def plan(cores, topo):
+    out, hops = {}, {}
+    for kind in ORDER:
+        for r in range(N):
+            src = cores[r]
+            group = [GR * (r // GR) + k if kind == "a" else GR * k + r % GR for k in range(GR)]
+            dsts = [cores[m] for m in group if m != r]
+            ways = (roads_a if kind == "a" else roads_b)(cores, src, dsts, topo)
+            for d in sorted(dsts, key=lambda d: -len(ways[d])):
+                way = [src] + ways[d] + [d]
+                for p, q in zip(way, way[1:]):
+                    key = (kind, slot(kind, r), q)
+                    if hops.get(key) != p:
+                        assert key not in hops
+                        hops[key] = p
+                        out.setdefault(p, {}).setdefault((kind, r), []).append(q)
+    return out, hops
+
+
+def masks(core, dsts, topo):
+    off, on = 0, 0
+    for d in dsts:
+        if topo.chip(d) != topo.chip(core):
+            off |= topo.mask(core, d)
+        else:
+            on |= topo.mask(core, d)
+    return off, (on & ~off) or on
+
+
+def rank_program(g, core, T, topo):
+    out, hops = plan(T.cores, topo)
+    rank = T.rank_of(core)
+    sem = T.sem
+
+    def landed(kind, k):
+        src = hops.get((kind, k, core))
+        if src is None:
+            return 0
+        dsts = [ds for (q, r), ds in out[src].items() if q == kind and slot(q, r) == k and core in ds][0]
+        off, on = masks(src, dsts, topo)
+        return engines(on if topo.chip(src) == topo.chip(core) else off)
+
+    if rank is not None:
+        compute(g, core, rank, T, landed, hops)
+
+    mine = out.get(core, {})
+    order = [t for t in mine if rank is not None and t[1] == rank]
+    order += [t for t in mine if t not in order]
+    sent = 0
+    for kind, r in order:
+        k, dsts = slot(kind, r), mine[(kind, r)]
+        off, on = masks(core, dsts, topo)
+        made = r == rank
+        if made:
+            g.wait_ge(sem["q" + kind], 1)
+        for part in "cs":
+            name = "%s%s%d" % (kind, part, k)
+            if not made:
+                g.wait_ge(sem[name], landed(kind, k))
+            v = T[name][:].bitcast(dt.uint8) if part == "c" else T[name][:]
+            ts = []
+            for away, mask in ((True, off), (False, on)):
+                ds = [d for d in dsts if (topo.chip(d) != topo.chip(core)) == away]
+                if ds:
+                    ts.append((ds, mask))
+                    sent += engines(mask)
+            if len(ts) == 1 and len(ts[0][0]) == 1:
+                rid, pid, _s = topo.addr(ts[0][0][0])
+                g.remote_dma(v, v, sem[name], sem.sent, pid, rid, ts[0][1])
+            else:
+                g.remote_dma_fused([RemoteDMATransfer(
+                    dst_ids=[DstId(rid=topo.addr(d)[0], pnc=topo.addr(d)[1]) for d in ds],
+                    dma_engine_mask=mask, remote_sem=sem[name], srcs=[v], dsts=[v for d in ds]) for ds, mask in ts],
+                    local_sem=sem.sent)
+    if sent:
+        g.wait_ge(sem.sent, sent)
+
+
+def compute(g, core, rank, T, landed, hops):
+    sem = T.sem
+
+    queues = [g.sync, g.scalar]
+    for q in ORDER:
+        cut = 512 * FIRST
+        for name, dst, src in (("lx", T["tx" + q][:], T["x" + q][:]),
+                               ("lw0", T["tw" + q][:, 0:cut], T["w" + q][:, 0:cut]),
+                               ("lw1", T["tw" + q][:, cut:512 * G], T["w" + q][:, cut:512 * G])):
+            queues[0].dma_start(dst, src).then_inc(sem[name + q], 16)
+            queues.reverse()
+
+    for q in ORDER:
+        n = COLS[q]
+        ps, t, k = T["ps" + q], T["t" + q], slot(q, rank)
+        g.vector.wait_ge(sem["lx" + q], 16)
+        g.vector.quantize_mx(T["cx" + q][:], T["sx" + q][:], T["tx" + q][:]).then_inc(sem["qx" + q], 1)
+        g.tensor.wait_ge(sem["qx" + q], 1)
+        for i in range(G):
+            if i == 0:
+                g.vector.wait_ge(sem["lw0" + q], 16)
+            if i == FIRST:
+                g.vector.wait_ge(sem["lw1" + q], 16)
+            c = slice(128 * i, 128 * i + 128)
+            qw, mm = sem["qw%s%d" % (q, i)], sem["mm%s%d" % (q, i)]
+            g.vector.quantize_mx(T["cw" + q][:, c], T["sw" + q][:, c],
+                                 T["tw" + q][:, 512 * i:512 * i + 512]).then_inc(qw, 1)
+            g.tensor.wait_ge(qw, 1)
+            z = ps[:, 512 * i:512 * i + n]
+            g.tensor.matmul_mx(z, T["cw" + q][:, c], T["sw" + q][:, c], T["cx" + q][:], T["sx" + q][:],
+                               True, True).then_inc(mm, 1)
+            if i < G - 1:
+                g.scalar.wait_ge(mm, 1)
+                g.scalar.activation(t[:, i:4 * n:4], z, ActivationFunctionType.Relu,
+                                    scale=SCALE).then_inc(sem["act" + q], 1)
+            else:
+                g.vector.wait_ge(mm, 1)
+                g.vector.tensor_scalar(t[:, i:4 * n:4], z, 0.0, SCALE, AluOpType.max,
+                                       AluOpType.mult).then_inc(sem["act" + q], 1)
+        g.vector.wait_ge(sem["act" + q], G)
+        g.vector.quantize_mx(T["%sc%d" % (q, k)][:], T["%ss%d" % (q, k)][:], t[:]).then_inc(sem["q" + q], 1)
+
+    def hop_count(kind, k):
+        n, c = 0, core
+        while (kind, k, c) in hops:
+            n, c = n + 1, hops[(kind, k, c)]
+        return n
+
+    ks = sorted(range(GR), key=lambda k: max((2 * hop_count(q, k) + ORDER.index(q) for q in "ab")))
+    g.tensor.wait_ge(sem.qa, 1)
+    g.tensor.wait_ge(sem.qb, 1)
+    y = T.psb[:, 0:256]
+    for n, k in enumerate(ks):
+        for q in "ab":
+            if landed(q, k):
+                for part in "cs":
+                    g.tensor.wait_ge(sem["%s%s%d" % (q, part, k)], landed(q, k))
+        m = g.tensor.matmul_mx(y, T["ac%d" % k][:], T["as%d" % k][:], T["bc%d" % k][:], T["bs%d" % k][:],
+                               n == 0, n == GR - 1)
+        if n == GR - 1:
+            m.then_inc(sem.mmy, 1)
+    g.vector.wait_ge(sem.mmy, 1)
+    g.vector.tensor_copy(T.ysb[:], y).then_inc(sem.cpy, 1)
+    g.sync.wait_ge(sem.cpy, 1)
+    g.sync.dma_start(T.y[:], T.ysb[:]).then_inc(sem.sty, 16)
+    g.sync.wait_ge(sem.sty, 16)

@@ -5,12 +5,12 @@ N, G, GR = 16, 4, 4
 SIM_CORES = 128
 SCALE = 0.031
 COLS = {"a": 128, "b": 256}
-FIRST = 3
-RELAYED = 2
+CUT = (0, 2)
 ORDER = "ab"
+SLOTS = {"a": GR + 1, "b": GR}
 
 SCRATCH = {"ysb": ("sbuf", [128, 256], "float32")}
-SEMAPHORES = ["sent", "mmy", "cpy", "sty"]
+SEMAPHORES = ["sent", "mmh", "acth"] + ["%s%d" % (s, u) for s in ("mmy", "cpy", "sty") for u in range(2)]
 for _q in "ab":
     _n = COLS[_q]
     SCRATCH["tx" + _q] = ("sbuf", [128, 4 * _n], "bfloat16")
@@ -21,16 +21,20 @@ for _q in "ab":
     SCRATCH["sw" + _q] = ("sbuf", [128, 128 * G], "uint8")
     SCRATCH["t" + _q] = ("sbuf", [128, 4 * _n], "bfloat16")
     SCRATCH["ps" + _q] = ("psum", [128, 512 * G], "float32")
-    for _k in range(GR):
+    for _k in range(SLOTS[_q]):
         SCRATCH["%sc%d" % (_q, _k)] = ("sbuf", [128, _n], "float8_e4m3fn_x4")
         SCRATCH["%ss%d" % (_q, _k)] = ("sbuf", [128, _n], "uint8")
         SEMAPHORES += ["%sc%d" % (_q, _k), "%ss%d" % (_q, _k)]
-    SEMAPHORES += [s + _q for s in ("lx", "lw0", "lw1", "qx", "act", "q")]
+    SEMAPHORES += [s + _q for s in ("lx", "qx", "act", "q")] + ["lw%d%s" % (_m, _q) for _m in range(len(CUT))]
     SEMAPHORES += ["%s%s%d" % (s, _q, i) for s in ("qw", "mm") for i in range(G)]
 
 
-def slot(kind, r):
-    return r % GR if kind == "a" else r // GR
+def place(kind, r, core, cores, topo):
+    if kind == "b":
+        return r // GR
+    if core not in cores and topo.chip(core) != topo.chip(cores[r]):
+        return GR
+    return r % GR
 
 
 def engines(mask):
@@ -48,18 +52,24 @@ def far(ranks, src, dst, topo):
             and topo.may_write(h, dst)]
 
 
-def roads_a(ranks, src, dsts, topo):
+def roads_a(ranks, src, dsts, topo, busy, taken):
+    ways = {}
+    last = dsts[-1]
+    if topo.may_write(src, last):
+        ways[last] = []
+    else:
+        hs = far(ranks, src, last, topo)
+        ways[last] = ([h for h in hs if h not in taken] or hs)[:1]
+        taken += ways[last]
     away = [d for d in dsts if not topo.same_plane(topo.chip(src), topo.chip(d))]
-    rest = [d for d in dsts if d not in away]
-    by = {}
-    for d in away + rest:
-        hs = [h for h in near(ranks, src, d, topo) if h not in by.values()]
+    used = []
+    for d in sorted(dsts[:-1], key=lambda d: d not in away):
+        hs = [h for h in near(ranks, src, d, topo) if h not in busy]
+        hs = [h for h in hs if h not in used] or hs
         hs.sort(key=lambda h: (away != [] and topo.may_write(h, away[0])) != (d in away))
-        if hs and len(by) < RELAYED:
-            by[d] = hs[0]
-        elif not topo.may_write(src, d):
-            by[d] = far(ranks, src, d, topo)[0]
-    return {d: [by[d]] if d in by else [] for d in dsts}
+        ways[d] = hs[:1]
+        used += hs[:1]
+    return ways
 
 
 def roads_b(ranks, src, dsts, topo):
@@ -68,30 +78,66 @@ def roads_b(ranks, src, dsts, topo):
         if topo.chip(d) == topo.chip(src):
             ways[d] = []
         elif topo.die(d) == topo.die(src):
-            ways[d] = [] if topo.may_write(src, d) else [near(ranks, src, d, topo)[0]]
+            ways[d] = [] if topo.may_write(src, d) else near(ranks, src, d, topo)[:1]
         else:
-            twin = [e for e in dsts if e != d and topo.chip(e) == topo.chip(d)][0]
-            ways[d] = [twin] if topo.may_write(src, d) else [far(ranks, src, d, topo)[0]]
+            twin = [e for e in dsts if e != d and topo.chip(e) == topo.chip(d)]
+            ways[d] = twin if topo.may_write(src, d) else far(ranks, src, d, topo)[:1]
     return ways
 
 
+def row_peers(r, way):
+    return [GR * (r // GR) + (r + way * x) % GR for x in range(1, GR)]
+
+
 def plan(cores, topo):
-    out, hops = {}, {}
+    sends, hops, taken = {}, {}, []
+    b_dsts = {r: [cores[(r + GR * x) % N] for x in range(1, GR)] for r in range(N)}
+    b_ways = {r: roads_b(cores, cores[r], b_dsts[r], topo) for r in range(N)}
+    b_relays = {r: [h for w in b_ways[r].values() for h in w if h not in cores] for r in range(N)}
+    carriers = [h for hs in b_relays.values() for h in hs]
+
+    def shared(row, way):
+        n = 0
+        for r in range(GR * row, GR * row + GR):
+            last = cores[row_peers(r, way)[-1]]
+            if not topo.may_write(cores[r], last) and far(cores, cores[r], last, topo)[0] in carriers:
+                n += 1
+        return n
+
     for kind in ORDER:
         for r in range(N):
             src = cores[r]
-            group = [GR * (r // GR) + k if kind == "a" else GR * k + r % GR for k in range(GR)]
-            dsts = [cores[m] for m in group if m != r]
-            ways = (roads_a if kind == "a" else roads_b)(cores, src, dsts, topo)
-            for d in sorted(dsts, key=lambda d: -len(ways[d])):
+            if kind == "a":
+                way = max((1, -1), key=lambda w: shared(r // GR, w))
+                dsts = [cores[m] for m in row_peers(r, way)]
+                ways = roads_a(cores, src, dsts, topo, b_relays[r], taken)
+            else:
+                dsts, ways = b_dsts[r], b_ways[r]
+            first = {d: (ways[d] + [d])[0] for d in dsts}
+
+            def late(d):
+                if topo.chip(first[d]) != topo.chip(src):
+                    return False
+                return kind == "a" or d == first[d] and any(not topo.may_write(src, e) for e in dsts)
+
+            for d in sorted(dsts, key=lambda d: (late(d), -len(ways[d]))):
                 way = [src] + ways[d] + [d]
                 for p, q in zip(way, way[1:]):
-                    key = (kind, slot(kind, r), q)
-                    if hops.get(key) != p:
-                        assert key not in hops
-                        hops[key] = p
-                        out.setdefault(p, {}).setdefault((kind, r), []).append(q)
-    return out, hops
+                    key = (kind, r, q)
+                    if key in hops:
+                        continue
+                    mine = sends.setdefault(p, [])
+                    entry = [e for e in mine if e[:2] == [kind, r] and e[3] == (p == src and late(d))]
+                    if not entry:
+                        entry = [[kind, r, [], p == src and late(d)]]
+                        mine.append(entry[0])
+                    entry[0][2].append(q)
+                    hops[key] = (p, entry[0])
+    at = [(kind, place(kind, r, q, cores, topo), q) for kind, r, q in hops]
+    assert len(at) == len(set(at))
+    for c, mine in sends.items():
+        mine.sort(key=lambda e: cores[e[1]] != c)
+    return sends, hops
 
 
 def masks(core, dsts, topo):
@@ -104,118 +150,152 @@ def masks(core, dsts, topo):
     return off, (on & ~off) or on
 
 
+def entry_masks(core, entry, everything, topo):
+    off, on = masks(core, entry[2], topo)
+    if entry[0] == "a":
+        alloff = masks(core, [d for e in everything for d in e[2]], topo)[0]
+        on = (on & ~alloff) or on
+    return off, on
+
+
 def rank_program(g, core, T, topo):
-    out, hops = plan(T.cores, topo)
+    cores = T.cores
+    sends, hops = plan(cores, topo)
     rank = T.rank_of(core)
     sem = T.sem
 
-    def landed(kind, k):
-        src = hops.get((kind, k, core))
-        if src is None:
+    def name(kind, part, r, c):
+        return "%s%s%d" % (kind, part, place(kind, r, c, cores, topo))
+
+    def landed(kind, r):
+        if (kind, r, core) not in hops:
             return 0
-        dsts = [ds for (q, r), ds in out[src].items() if q == kind and slot(q, r) == k and core in ds][0]
-        off, on = masks(src, dsts, topo)
+        src, entry = hops[(kind, r, core)]
+        off, on = entry_masks(src, entry, sends[src], topo)
         return engines(on if topo.chip(src) == topo.chip(core) else off)
 
     if rank is not None:
         compute(g, core, rank, T, landed, hops)
 
-    mine = out.get(core, {})
-    order = [t for t in mine if rank is not None and t[1] == rank]
-    order += [t for t in mine if t not in order]
+    calls = [(entry, part) for entry in sends.get(core, []) for part in "cs"]
+    own_a = [c for c in calls if c[0][0] == "a" and c[0][1] == rank]
+    calls = sorted(own_a, key=lambda c: c[1] == "s") + [c for c in calls if c not in own_a]
     sent = 0
-    for kind, r in order:
-        k, dsts = slot(kind, r), mine[(kind, r)]
-        off, on = masks(core, dsts, topo)
-        made = r == rank
-        if made:
-            g.wait_ge(sem["q" + kind], 1)
-        for part in "cs":
-            name = "%s%s%d" % (kind, part, k)
-            if not made:
-                g.wait_ge(sem[name], landed(kind, k))
-            v = T[name][:].bitcast(dt.uint8) if part == "c" else T[name][:]
-            ts = []
-            for away, mask in ((True, off), (False, on)):
-                ds = [d for d in dsts if (topo.chip(d) != topo.chip(core)) == away]
-                if ds:
-                    ts.append((ds, mask))
-                    sent += engines(mask)
-            if len(ts) == 1 and len(ts[0][0]) == 1:
-                rid, pid, _s = topo.addr(ts[0][0][0])
-                g.remote_dma(v, v, sem[name], sem.sent, pid, rid, ts[0][1])
-            else:
-                g.remote_dma_fused([RemoteDMATransfer(
-                    dst_ids=[DstId(rid=topo.addr(d)[0], pnc=topo.addr(d)[1]) for d in ds],
-                    dma_engine_mask=mask, remote_sem=sem[name], srcs=[v], dsts=[v for d in ds]) for ds, mask in ts],
-                    local_sem=sem.sent)
+    for entry, part in calls:
+        kind, r, dsts, _late = entry
+        off, on = entry_masks(core, entry, sends[core], topo)
+        mine = name(kind, part, r, core)
+        if r == rank:
+            g.wait_ge(sem["q" + kind], 1 if kind == "a" else 2)
+        else:
+            g.wait_ge(sem[mine], landed(kind, r))
+
+        def view(c):
+            t = T[name(kind, part, r, c)]
+            return t[:].bitcast(dt.uint8) if part == "c" else t[:]
+
+        ts = []
+        for away, mask in ((True, off), (False, on)):
+            ds = [d for d in dsts if (topo.chip(d) != topo.chip(core)) == away]
+            if ds:
+                assert len(set(name(kind, part, r, d) for d in ds)) == 1
+                ts.append((ds, mask))
+                sent += engines(mask)
+        if len(ts) == 1 and len(ts[0][0]) == 1:
+            d = ts[0][0][0]
+            rid, pid, _s = topo.addr(d)
+            g.remote_dma(view(d), view(core), sem[name(kind, part, r, d)], sem.sent, pid, rid, ts[0][1])
+        else:
+            g.remote_dma_fused([RemoteDMATransfer(
+                dst_ids=[DstId(rid=topo.addr(d)[0], pnc=topo.addr(d)[1]) for d in ds],
+                dma_engine_mask=mask, remote_sem=sem[name(kind, part, r, ds[0])], srcs=[view(core)],
+                dsts=[view(d) for d in ds]) for ds, mask in ts], local_sem=sem.sent)
     if sent:
         g.wait_ge(sem.sent, sent)
 
 
 def compute(g, core, rank, T, landed, hops):
     sem = T.sem
+    own = {"a": rank % GR, "b": rank // GR}
 
     queues = [g.sync, g.scalar]
     for q in ORDER:
-        cut = 512 * FIRST
-        for name, dst, src in (("lx", T["tx" + q][:], T["x" + q][:]),
-                               ("lw0", T["tw" + q][:, 0:cut], T["w" + q][:, 0:cut]),
-                               ("lw1", T["tw" + q][:, cut:512 * G], T["w" + q][:, cut:512 * G])):
-            queues[0].dma_start(dst, src).then_inc(sem[name + q], 16)
+        jobs = [("lx" + q, T["tx" + q][:], T["x" + q][:])]
+        for m, (u, v) in enumerate(zip(CUT, CUT[1:] + (G,))):
+            jobs.append(("lw%d%s" % (m, q), T["tw" + q][:, 512 * u:512 * v], T["w" + q][:, 512 * u:512 * v]))
+        for name, dst, src in jobs:
+            queues[0].dma_start(dst, src).then_inc(sem[name], 16)
             queues.reverse()
+
+    def scalar_act(out, z, after, done):
+        g.scalar.wait_ge(after, 1)
+        g.scalar.activation(out, z, ActivationFunctionType.Relu, scale=SCALE).then_inc(done, 1)
+
+    def vector_act(out, z, after, done):
+        g.vector.wait_ge(after, 1)
+        g.vector.tensor_scalar(out, z, 0.0, SCALE, AluOpType.max, AluOpType.mult).then_inc(done, 1)
 
     for q in ORDER:
         n = COLS[q]
-        ps, t, k = T["ps" + q], T["t" + q], slot(q, rank)
+        ps, t, act = T["ps" + q], T["t" + q], sem["act" + q]
+        cx, sx, cw, sw = T["cx" + q], T["sx" + q], T["cw" + q], T["sw" + q]
+        own_c, own_s = T["%sc%d" % (q, own[q])], T["%ss%d" % (q, own[q])]
         g.vector.wait_ge(sem["lx" + q], 16)
-        g.vector.quantize_mx(T["cx" + q][:], T["sx" + q][:], T["tx" + q][:]).then_inc(sem["qx" + q], 1)
+        g.vector.quantize_mx(cx[:], sx[:], T["tx" + q][:]).then_inc(sem["qx" + q], 1)
         g.tensor.wait_ge(sem["qx" + q], 1)
+        zs = [ps[:, 512 * i:512 * i + n] for i in range(G)]
+        mms = [sem["mm%s%d" % (q, i)] for i in range(G)]
         for i in range(G):
-            if i == 0:
-                g.vector.wait_ge(sem["lw0" + q], 16)
-            if i == FIRST:
-                g.vector.wait_ge(sem["lw1" + q], 16)
             c = slice(128 * i, 128 * i + 128)
-            qw, mm = sem["qw%s%d" % (q, i)], sem["mm%s%d" % (q, i)]
-            g.vector.quantize_mx(T["cw" + q][:, c], T["sw" + q][:, c],
-                                 T["tw" + q][:, 512 * i:512 * i + 512]).then_inc(qw, 1)
+            qw = sem["qw%s%d" % (q, i)]
+            if i in CUT:
+                g.vector.wait_ge(sem["lw%d%s" % (CUT.index(i), q)], 16)
+            g.vector.quantize_mx(cw[:, c], sw[:, c], T["tw" + q][:, 512 * i:512 * i + 512]).then_inc(qw, 1)
             g.tensor.wait_ge(qw, 1)
-            z = ps[:, 512 * i:512 * i + n]
-            g.tensor.matmul_mx(z, T["cw" + q][:, c], T["sw" + q][:, c], T["cx" + q][:], T["sx" + q][:],
-                               True, True).then_inc(mm, 1)
-            if i < G - 1:
-                g.scalar.wait_ge(mm, 1)
-                g.scalar.activation(t[:, i:4 * n:4], z, ActivationFunctionType.Relu,
-                                    scale=SCALE).then_inc(sem["act" + q], 1)
-            else:
-                g.vector.wait_ge(mm, 1)
-                g.vector.tensor_scalar(t[:, i:4 * n:4], z, 0.0, SCALE, AluOpType.max,
-                                       AluOpType.mult).then_inc(sem["act" + q], 1)
-        g.vector.wait_ge(sem["act" + q], G)
-        g.vector.quantize_mx(T["%sc%d" % (q, k)][:], T["%ss%d" % (q, k)][:], t[:]).then_inc(sem["q" + q], 1)
+            if q == "b" and i == G - 1:
+                break
+            g.tensor.matmul_mx(zs[i], cw[:, c], sw[:, c], cx[:], sx[:], True, True).then_inc(mms[i], 1)
+            if i < (G - 1 if q == "a" else G - 2):
+                scalar_act(t[:, i:4 * n:4], zs[i], mms[i], act)
+        if q == "a":
+            vector_act(t[:, 3:4 * n:4], zs[3], mms[3], act)
+            g.vector.wait_ge(act, G)
+            g.vector.quantize_mx(own_c[:], own_s[:], t[:]).then_inc(sem.qa, 1)
+            continue
+        vector_act(t[:, 2:4 * n:4], zs[2], mms[2], act)
+        h = n // 2
+        for m, (z, after, done) in enumerate(((ps[:, 512 * 3:512 * 3 + h], mms[3], act), (T.psa[:, 0:h], sem.mmh, sem.acth))):
+            x, e = slice(h * m, h * m + h), slice(4 * h * m, 4 * h * m + 4 * h)
+            g.tensor.matmul_mx(z, cw[:, c], sw[:, c], cx[:, x], sx[:, x], True, True).then_inc(after, 1)
+            scalar_act(t[:, 4 * h * m + 3:4 * h * m + 4 * h:4], z, after, done)
+            g.vector.wait_ge(done, 1 if m else G)
+            g.vector.quantize_mx(own_c[:, x], own_s[:, x], t[:, e]).then_inc(sem.qb, 1)
 
-    def hop_count(kind, k):
+    def travel(kind, r):
         n, c = 0, core
-        while (kind, k, c) in hops:
-            n, c = n + 1, hops[(kind, k, c)]
-        return n
+        while (kind, r, c) in hops:
+            n, c = n + (2 if T.rank_of(c) is not None else 2.5), hops[(kind, r, c)][0]
+        return n + ORDER.index(kind)
 
-    ks = sorted(range(GR), key=lambda k: max((2 * hop_count(q, k) + ORDER.index(q) for q in "ab")))
+    slices = [(k, {"a": GR * (rank // GR) + k, "b": GR * k + rank % GR}) for k in range(GR)]
+    slices.sort(key=lambda s: max(travel(q, r) for q, r in s[1].items()))
     g.tensor.wait_ge(sem.qa, 1)
-    g.tensor.wait_ge(sem.qb, 1)
-    y = T.psb[:, 0:256]
-    for n, k in enumerate(ks):
-        for q in "ab":
-            if landed(q, k):
+    g.tensor.wait_ge(sem.qb, 2)
+    halves = [(T.psb[:, 512 * u:512 * u + 128], slice(128 * u, 128 * u + 128)) for u in range(2)]
+    for n, (k, makers) in enumerate(slices):
+        for q, r in makers.items():
+            if landed(q, r):
                 for part in "cs":
-                    g.tensor.wait_ge(sem["%s%s%d" % (q, part, k)], landed(q, k))
-        m = g.tensor.matmul_mx(y, T["ac%d" % k][:], T["as%d" % k][:], T["bc%d" % k][:], T["bs%d" % k][:],
-                               n == 0, n == GR - 1)
-        if n == GR - 1:
-            m.then_inc(sem.mmy, 1)
-    g.vector.wait_ge(sem.mmy, 1)
-    g.vector.tensor_copy(T.ysb[:], y).then_inc(sem.cpy, 1)
-    g.sync.wait_ge(sem.cpy, 1)
-    g.sync.dma_start(T.y[:], T.ysb[:]).then_inc(sem.sty, 16)
-    g.sync.wait_ge(sem.sty, 16)
+                    g.tensor.wait_ge(sem["%s%s%d" % (q, part, k)], landed(q, r))
+        a_c, a_s, b_c, b_s = [T["%s%s%d" % (q, part, k)] for q in "ab" for part in "cs"]
+        for u, (z, c) in enumerate(halves):
+            m = g.tensor.matmul_mx(z, a_c[:], a_s[:], b_c[:, c], b_s[:, c], n == 0, n == GR - 1)
+            if n == GR - 1:
+                m.then_inc(sem["mmy%d" % u], 1)
+    for u, (z, c) in enumerate(halves):
+        queue = (g.sync, g.scalar)[u]
+        g.vector.wait_ge(sem["mmy%d" % u], 1)
+        g.vector.tensor_copy(T.ysb[:, c], z).then_inc(sem["cpy%d" % u], 1)
+        queue.wait_ge(sem["cpy%d" % u], 1)
+        queue.dma_start(T.y[:, c], T.ysb[:, c]).then_inc(sem["sty%d" % u], 16)
+        queue.wait_ge(sem["sty%d" % u], 16)

from concourse.bass import DstId, RemoteDMATransfer
from concourse.mybir import dt, AluOpType, ActivationFunctionType

N, G, GR = 16, 4, 4
SIM_CORES = 128
SCALE = 0.031
COLS = {"a": 128, "b": 256}
CUT = (0, 2)
ORDER = "ab"
SLOTS = {"a": GR + 1, "b": GR}

SCRATCH = {"ysb": ("sbuf", [128, 256], "float32")}
SEMAPHORES = ["sent", "mmh", "acth"] + ["%s%d" % (s, u) for s in ("mmy", "cpy", "sty") for u in range(2)]
for _q in "ab":
    _n = COLS[_q]
    SCRATCH["tx" + _q] = ("sbuf", [128, 4 * _n], "bfloat16")
    SCRATCH["tw" + _q] = ("sbuf", [128, 512 * G], "bfloat16")
    SCRATCH["cx" + _q] = ("sbuf", [128, _n], "float8_e4m3fn_x4")
    SCRATCH["sx" + _q] = ("sbuf", [128, _n], "uint8")
    SCRATCH["cw" + _q] = ("sbuf", [128, 128 * G], "float8_e4m3fn_x4")
    SCRATCH["sw" + _q] = ("sbuf", [128, 128 * G], "uint8")
    SCRATCH["t" + _q] = ("sbuf", [128, 4 * _n], "bfloat16")
    SCRATCH["ps" + _q] = ("psum", [128, 512 * G], "float32")
    for _k in range(SLOTS[_q]):
        SCRATCH["%sc%d" % (_q, _k)] = ("sbuf", [128, _n], "float8_e4m3fn_x4")
        SCRATCH["%ss%d" % (_q, _k)] = ("sbuf", [128, _n], "uint8")
        SEMAPHORES += ["%sc%d" % (_q, _k), "%ss%d" % (_q, _k)]
    SEMAPHORES += [s + _q for s in ("lx", "qx", "act", "q")] + ["lw%d%s" % (_m, _q) for _m in range(len(CUT))]
    SEMAPHORES += ["%s%s%d" % (s, _q, i) for s in ("qw", "mm") for i in range(G)]


def place(kind, r, core, cores, topo):
    if kind == "b":
        return r // GR
    if core not in cores and topo.chip(core) != topo.chip(cores[r]):
        return GR
    return r % GR


def engines(mask):
    return bin(mask).count("1")


def near(ranks, src, dst, topo):
    return [h for h in range(SIM_CORES) if h not in ranks and topo.chip(h) == topo.chip(src)
            and topo.die(h) == topo.die(src) and topo.may_write(h, dst)]


def far(ranks, src, dst, topo):
    return [h for h in range(SIM_CORES) if h not in ranks and topo.mates(topo.chip(h), topo.chip(dst))
            and topo.same_plane(topo.chip(h), topo.chip(src)) and topo.die(h) == topo.die(src)
            and topo.may_write(h, dst)]


def roads_a(ranks, src, dsts, topo, busy, taken):
    ways = {}
    last = dsts[-1]
    if topo.may_write(src, last):
        ways[last] = []
    else:
        hs = far(ranks, src, last, topo)
        ways[last] = ([h for h in hs if h not in taken] or hs)[:1]
        taken += ways[last]
    away = [d for d in dsts if not topo.same_plane(topo.chip(src), topo.chip(d))]
    used = []
    for d in sorted(dsts[:-1], key=lambda d: d not in away):
        hs = [h for h in near(ranks, src, d, topo) if h not in busy]
        hs = [h for h in hs if h not in used] or hs
        hs.sort(key=lambda h: (away != [] and topo.may_write(h, away[0])) != (d in away))
        ways[d] = hs[:1]
        used += hs[:1]
    return ways


def roads_b(ranks, src, dsts, topo):
    ways = {}
    for d in dsts:
        if topo.chip(d) == topo.chip(src):
            ways[d] = []
        elif topo.die(d) == topo.die(src):
            ways[d] = [] if topo.may_write(src, d) else near(ranks, src, d, topo)[:1]
        else:
            twin = [e for e in dsts if e != d and topo.chip(e) == topo.chip(d)]
            ways[d] = twin if topo.may_write(src, d) else far(ranks, src, d, topo)[:1]
    return ways


def row_peers(r, way):
    return [GR * (r // GR) + (r + way * x) % GR for x in range(1, GR)]


def plan(cores, topo):
    sends, hops, taken = {}, {}, []
    b_dsts = {r: [cores[(r + GR * x) % N] for x in range(1, GR)] for r in range(N)}
    b_ways = {r: roads_b(cores, cores[r], b_dsts[r], topo) for r in range(N)}
    b_relays = {r: [h for w in b_ways[r].values() for h in w if h not in cores] for r in range(N)}
    carriers = [h for hs in b_relays.values() for h in hs]

    def shared(row, way):
        n = 0
        for r in range(GR * row, GR * row + GR):
            last = cores[row_peers(r, way)[-1]]
            if not topo.may_write(cores[r], last) and far(cores, cores[r], last, topo)[0] in carriers:
                n += 1
        return n

    for kind in ORDER:
        for r in range(N):
            src = cores[r]
            if kind == "a":
                way = max((1, -1), key=lambda w: shared(r // GR, w))
                dsts = [cores[m] for m in row_peers(r, way)]
                ways = roads_a(cores, src, dsts, topo, b_relays[r], taken)
            else:
                dsts, ways = b_dsts[r], b_ways[r]
            first = {d: (ways[d] + [d])[0] for d in dsts}

            def late(d):
                if topo.chip(first[d]) != topo.chip(src):
                    return False
                return kind == "a" or d == first[d] and any(not topo.may_write(src, e) for e in dsts)

            for d in sorted(dsts, key=lambda d: (late(d), -len(ways[d]))):
                way = [src] + ways[d] + [d]
                for p, q in zip(way, way[1:]):
                    key = (kind, r, q)
                    if key in hops:
                        continue
                    mine = sends.setdefault(p, [])
                    entry = [e for e in mine if e[:2] == [kind, r] and e[3] == (p == src and late(d))]
                    if not entry:
                        entry = [[kind, r, [], p == src and late(d)]]
                        mine.append(entry[0])
                    entry[0][2].append(q)
                    hops[key] = (p, entry[0])
    at = [(kind, place(kind, r, q, cores, topo), q) for kind, r, q in hops]
    assert len(at) == len(set(at))
    for c, mine in sends.items():
        mine.sort(key=lambda e: cores[e[1]] != c)
    return sends, hops


def masks(core, dsts, topo):
    off, on = 0, 0
    for d in dsts:
        if topo.chip(d) != topo.chip(core):
            off |= topo.mask(core, d)
        else:
            on |= topo.mask(core, d)
    return off, (on & ~off) or on


def entry_masks(core, entry, everything, topo):
    off, on = masks(core, entry[2], topo)
    if entry[0] == "a":
        alloff = masks(core, [d for e in everything for d in e[2]], topo)[0]
        on = (on & ~alloff) or on
    return off, on


def rank_program(g, core, T, topo):
    cores = T.cores
    sends, hops = plan(cores, topo)
    rank = T.rank_of(core)
    sem = T.sem

    def name(kind, part, r, c):
        return "%s%s%d" % (kind, part, place(kind, r, c, cores, topo))

    def landed(kind, r):
        if (kind, r, core) not in hops:
            return 0
        src, entry = hops[(kind, r, core)]
        off, on = entry_masks(src, entry, sends[src], topo)
        return engines(on if topo.chip(src) == topo.chip(core) else off)

    if rank is not None:
        compute(g, core, rank, T, landed, hops)

    calls = [(entry, part) for entry in sends.get(core, []) for part in "cs"]
    own_a = [c for c in calls if c[0][0] == "a" and c[0][1] == rank]
    calls = sorted(own_a, key=lambda c: c[1] == "s") + [c for c in calls if c not in own_a]
    sent = 0
    for entry, part in calls:
        kind, r, dsts, _late = entry
        off, on = entry_masks(core, entry, sends[core], topo)
        mine = name(kind, part, r, core)
        if r == rank:
            g.wait_ge(sem["q" + kind], 1 if kind == "a" else 2)
        else:
            g.wait_ge(sem[mine], landed(kind, r))

        def view(c):
            t = T[name(kind, part, r, c)]
            return t[:].bitcast(dt.uint8) if part == "c" else t[:]

        ts = []
        for away, mask in ((True, off), (False, on)):
            ds = [d for d in dsts if (topo.chip(d) != topo.chip(core)) == away]
            if ds:
                assert len(set(name(kind, part, r, d) for d in ds)) == 1
                ts.append((ds, mask))
                sent += engines(mask)
        if len(ts) == 1 and len(ts[0][0]) == 1:
            d = ts[0][0][0]
            rid, pid, _s = topo.addr(d)
            g.remote_dma(view(d), view(core), sem[name(kind, part, r, d)], sem.sent, pid, rid, ts[0][1])
        else:
            g.remote_dma_fused([RemoteDMATransfer(
                dst_ids=[DstId(rid=topo.addr(d)[0], pnc=topo.addr(d)[1]) for d in ds],
                dma_engine_mask=mask, remote_sem=sem[name(kind, part, r, ds[0])], srcs=[view(core)],
                dsts=[view(d) for d in ds]) for ds, mask in ts], local_sem=sem.sent)
    if sent:
        g.wait_ge(sem.sent, sent)


def compute(g, core, rank, T, landed, hops):
    sem = T.sem
    own = {"a": rank % GR, "b": rank // GR}

    queues = [g.sync, g.scalar]
    for q in ORDER:
        jobs = [("lx" + q, T["tx" + q][:], T["x" + q][:])]
        for m, (u, v) in enumerate(zip(CUT, CUT[1:] + (G,))):
            jobs.append(("lw%d%s" % (m, q), T["tw" + q][:, 512 * u:512 * v], T["w" + q][:, 512 * u:512 * v]))
        for name, dst, src in jobs:
            queues[0].dma_start(dst, src).then_inc(sem[name], 16)
            queues.reverse()

    def scalar_act(out, z, after, done):
        g.scalar.wait_ge(after, 1)
        g.scalar.activation(out, z, ActivationFunctionType.Relu, scale=SCALE).then_inc(done, 1)

    def vector_act(out, z, after, done):
        g.vector.wait_ge(after, 1)
        g.vector.tensor_scalar(out, z, 0.0, SCALE, AluOpType.max, AluOpType.mult).then_inc(done, 1)

    for q in ORDER:
        n = COLS[q]
        ps, t, act = T["ps" + q], T["t" + q], sem["act" + q]
        cx, sx, cw, sw = T["cx" + q], T["sx" + q], T["cw" + q], T["sw" + q]
        own_c, own_s = T["%sc%d" % (q, own[q])], T["%ss%d" % (q, own[q])]
        g.vector.wait_ge(sem["lx" + q], 16)
        g.vector.quantize_mx(cx[:], sx[:], T["tx" + q][:]).then_inc(sem["qx" + q], 1)
        g.tensor.wait_ge(sem["qx" + q], 1)
        zs = [ps[:, 512 * i:512 * i + n] for i in range(G)]
        mms = [sem["mm%s%d" % (q, i)] for i in range(G)]
        for i in range(G):
            c = slice(128 * i, 128 * i + 128)
            qw = sem["qw%s%d" % (q, i)]
            if i in CUT:
                g.vector.wait_ge(sem["lw%d%s" % (CUT.index(i), q)], 16)
            g.vector.quantize_mx(cw[:, c], sw[:, c], T["tw" + q][:, 512 * i:512 * i + 512]).then_inc(qw, 1)
            g.tensor.wait_ge(qw, 1)
            if q == "b" and i == G - 1:
                break
            g.tensor.matmul_mx(zs[i], cw[:, c], sw[:, c], cx[:], sx[:], True, True).then_inc(mms[i], 1)
            if i < (G - 1 if q == "a" else G - 2):
                scalar_act(t[:, i:4 * n:4], zs[i], mms[i], act)
        if q == "a":
            vector_act(t[:, 3:4 * n:4], zs[3], mms[3], act)
            g.vector.wait_ge(act, G)
            g.vector.quantize_mx(own_c[:], own_s[:], t[:]).then_inc(sem.qa, 1)
            continue
        vector_act(t[:, 2:4 * n:4], zs[2], mms[2], act)
        h = n // 2
        for m, (z, after, done) in enumerate(((ps[:, 512 * 3:512 * 3 + h], mms[3], act), (T.psa[:, 0:h], sem.mmh, sem.acth))):
            x, e = slice(h * m, h * m + h), slice(4 * h * m, 4 * h * m + 4 * h)
            g.tensor.matmul_mx(z, cw[:, c], sw[:, c], cx[:, x], sx[:, x], True, True).then_inc(after, 1)
            scalar_act(t[:, 4 * h * m + 3:4 * h * m + 4 * h:4], z, after, done)
            g.vector.wait_ge(done, 1 if m else G)
            g.vector.quantize_mx(own_c[:, x], own_s[:, x], t[:, e]).then_inc(sem.qb, 1)

    def travel(kind, r):
        n, c = 0, core
        while (kind, r, c) in hops:
            n, c = n + (2 if T.rank_of(c) is not None else 2.5), hops[(kind, r, c)][0]
        return n + ORDER.index(kind)

    slices = [(k, {"a": GR * (rank // GR) + k, "b": GR * k + rank % GR}) for k in range(GR)]
    slices.sort(key=lambda s: max(travel(q, r) for q, r in s[1].items()))
    g.tensor.wait_ge(sem.qa, 1)
    g.tensor.wait_ge(sem.qb, 2)
    halves = [(T.psb[:, 512 * u:512 * u + 128], slice(128 * u, 128 * u + 128)) for u in range(2)]
    for n, (k, makers) in enumerate(slices):
        for q, r in makers.items():
            if landed(q, r):
                for part in "cs":
                    g.tensor.wait_ge(sem["%s%s%d" % (q, part, k)], landed(q, r))
        a_c, a_s, b_c, b_s = [T["%s%s%d" % (q, part, k)] for q in "ab" for part in "cs"]
        for u, (z, c) in enumerate(halves):
            m = g.tensor.matmul_mx(z, a_c[:], a_s[:], b_c[:, c], b_s[:, c], n == 0, n == GR - 1)
            if n == GR - 1:
                m.then_inc(sem["mmy%d" % u], 1)
    for u, (z, c) in enumerate(halves):
        queue = (g.sync, g.scalar)[u]
        g.vector.wait_ge(sem["mmy%d" % u], 1)
        g.vector.tensor_copy(T.ysb[:, c], z).then_inc(sem["cpy%d" % u], 1)
        queue.wait_ge(sem["cpy%d" % u], 1)
        queue.dma_start(T.y[:, c], T.ysb[:, c]).then_inc(sem["sty%d" % u], 16)
        queue.wait_ge(sem["sty%d" % u], 16)
